import numpy as np
CORES = [0,4,1,5,2,6,3,7]
N = 8
def setup_inputs(rng):
    return {"x": rng.standard_normal((N, 128, 256), dtype=np.float32)}
def reference(x):
    m = x.max(axis=0)
    return {"y": x - m}

from concourse.bass import DstId, RemoteDMATransfer
from concourse.mybir import AluOpType

ROWS, COLS = 128, 256
NBLK = 4
W = COLS // NBLK
MAX = 2

SCRATCH = {
    "xs":   ("sbuf", [ROWS, COLS], "float32"),
    "land": ("sbuf", [ROWS, NBLK * W], "float32"),
    "part": ("sbuf", [ROWS, W], "float32"),
    "m":    ("sbuf", [ROWS, COLS], "float32"),
    "ys":   ("sbuf", [ROWS, COLS], "float32"),
}
SEMAPHORES = [
    "loaded",
    "piece",
    "half",
    "full",
    "sent",
    "done",
    "stored",
]


def blk(t, q):
    return t[:, q * W:(q + 1) * W]


def rank_program(g, core, T, topo):
    if T.rank_of(core) is None:
        return

    def dst(c):
        rid, pid, _se = topo.addr(c)
        return DstId(rid=rid, pnc=pid)

    mine = sorted(c for c in T.cores if topo.die(c) == topo.die(core))
    other = sorted(c for c in T.cores if topo.die(c) != topo.die(core))
    k = mine.index(core)
    partner = other[k]
    mates = [(j, c) for j, c in enumerate(mine) if c != core]
    S = T.sem

    g.sync.dma_start(T.xs[:], T.x[:]).then_inc(S.loaded, 16)

    g.wait_ge(S.loaded, 16)
    g.remote_dma_fused(
        [RemoteDMATransfer(dst_ids=[dst(c)], dma_engine_mask=0xF << (4 * n), remote_sem=S.piece,
                           src=blk(T.xs, j), dst=blk(T.land, k))
         for n, (j, c) in enumerate(mates)],
        local_sem=S.sent)

    die_versions = [blk(T.xs, k)] + [blk(T.land, j) for j, _c in mates]
    g.wait_ge(S.piece, 4 * len(mates))
    g.remote_dma_fused(
        [RemoteDMATransfer(dst_ids=[dst(partner)], dma_engine_mask=0xFFFF, remote_sem=S.half,
                           srcs=die_versions, dsts=[T.part[:]], alu_op=MAX)],
        local_sem=S.sent)

    takers = [c for _j, c in mates] + [partner]
    g.wait_ge(S.half, 16)
    g.remote_dma_fused(
        [RemoteDMATransfer(dst_ids=[dst(c) for c in takers], dma_engine_mask=0xFFFF, remote_sem=S.full,
                           srcs=die_versions + [T.part[:]], dsts=[blk(T.m, k) for _c in takers], alu_op=MAX)],
        local_sem=S.sent)

    g.vector.wait_ge(S.loaded, 16)
    g.vector.wait_ge(S.full, 16 * len(takers))
    g.vector.tensor_tensor(T.ys[:], T.xs[:], T.m[:], AluOpType.subtract).then_inc(S.done, 1)
    g.sync.wait_ge(S.done, 1)
    g.sync.dma_start(T.y[:], T.ys[:]).then_inc(S.stored, 16)
    g.sync.wait_ge(S.stored, 16)

    g.wait_ge(S.sent, 4 * len(mates) + 16 + 16)
